import numpy as np
import ml_dtypes


def mxq(x, axis, fmt="e4m3"):
    dtype, down = {"e4m3": (ml_dtypes.float8_e4m3fn, 7), "e5m2": (ml_dtypes.float8_e5m2, 14)}[fmt]
    v = np.moveaxis(np.asarray(x, np.float32).astype(ml_dtypes.bfloat16).astype(np.float64), axis, -1)
    blocks = v.reshape(v.shape[:-1] + (-1, 32))
    amax = np.abs(blocks).max(-1, keepdims=True)
    byte = np.maximum(np.where(amax > 0, np.frexp(amax)[1] - 1 + 127, 0) - down, 1)
    scale = np.exp2(byte - 127.0)
    codes = (blocks / scale).astype(np.float32).astype(dtype).astype(np.float64)
    return np.moveaxis((codes * scale).reshape(v.shape), -1, axis)


WIDE = False


def mx_kscale(k):
    if not WIDE:
        return np.ones(k)
    levels = np.array([30, -30])
    if k % 512:
        return np.exp2(np.random.permutation(np.resize(levels, k // 32))).repeat(32)
    a = np.empty((k // 512, 16))
    for p in range(k // 512):
        a[p, :8] = np.random.permutation(np.resize(levels, 8))
        for g in range(8):
            far = levels[np.abs(levels - a[p, g]) >= 10]
            a[p, g + 8] = far[np.random.randint(len(far))]
    return np.exp2(a.ravel()).repeat(32)


def f64(x):
    return np.asarray(x).astype(np.float64)


def striped(idx):
    return np.tile(np.asarray(idx).reshape(-1, 16).T, (8, 1)).astype(np.uint16)


def unstriped(offs):
    return offs[:16].T.reshape(-1).astype(np.int64)


def striped8(idx):
    return np.asarray(idx).reshape(8, -1, 16).transpose(0, 2, 1).reshape(128, -1).astype(np.uint16)


def unstriped8(offs):
    return offs.reshape(8, 16, -1).transpose(0, 2, 1).reshape(8, -1).astype(np.int64)


def pick8(x, idx, run):
    r = np.arange(len(x))
    return x[r[:, None], idx[r % (8 * run) // run]]


E2M1 = np.array([0.0, 0.5, 1.0, 1.5, 2.0, 3.0, 4.0, 6.0, -0.0, -0.5, -1.0, -1.5, -2.0, -3.0, -4.0, -6.0])


def pack_weight(w, fmt):
    k, n = w.shape
    w = f64(np.asarray(w, np.float32).astype(ml_dtypes.bfloat16)).reshape(k // 32, 32, n)
    amax = np.abs(w).max(1)
    if fmt in ("e4m3", "e5m2"):
        byte = np.frexp(amax)[1] - 1 + 127 - (7 if fmt == "e4m3" else 14)
    else:
        mant, ex = np.frexp(amax / 6.0)
        byte = np.where(mant > 0.5, ex, ex - 1) + 127
    byte = np.clip(np.where(amax > 0, byte, 1), 1, 254)
    scaled = (w * np.exp2(127.0 - byte)[:, None, :]).reshape(k, n).astype(np.float32)
    by_word = np.ascontiguousarray(scaled.reshape(k // 512, 128, 4, n).transpose(0, 1, 3, 2))
    if fmt in ("e4m3", "e5m2"):
        words = by_word.astype(ml_dtypes.float8_e4m3fn if fmt == "e4m3" else ml_dtypes.float8_e5m2).view(np.uint8)
    else:
        c = by_word.astype(ml_dtypes.float4_e2m1fn).view(np.uint8) & 0xF
        words = (c[..., 0::2] | (c[..., 1::2] << 4)).reshape(k // 512, 128, 2 * n)
    return np.ascontiguousarray(words), np.ascontiguousarray(byte.astype(np.uint8).reshape(k // 512, 16, n))


def unpack_weight(words, scales, fmt):
    g, _, n = scales.shape
    words = np.ascontiguousarray(words).reshape(g, 128, n, -1)
    if fmt in ("e4m3", "e5m2"):
        vals = words.view(ml_dtypes.float8_e4m3fn if fmt == "e4m3" else ml_dtypes.float8_e5m2).astype(np.float64)
    else:
        nib = np.empty((g, 128, n, 4), np.uint8)
        nib[..., 0::2] = words & 0xF
        nib[..., 1::2] = words >> 4
        vals = E2M1[nib]
    vals = vals * np.repeat(np.exp2(scales.astype(np.float64) - 127.0), 8, axis=1)[..., None]
    return vals.transpose(0, 1, 3, 2).reshape(g * 512, n)


K, T, J, R, G, N, C = 1024, 512, 256, 512, 128, 256, 1024


def setup_inputs():
    n = np.random.standard_normal
    idx = np.stack([np.random.permutation(T)[:J] for _ in range(8)])
    idx2 = np.random.permutation(C)[:G]
    fk = mx_kscale(K)
    fr = mx_kscale(R)
    xtp = pack_weight(n((K, T)) / fk[:, None], "e4m3")
    wp = pack_weight(n((K, R)) * 1 / np.sqrt(K) * fk[:, None] * fr, "e2m1")
    wbp = pack_weight(n((R, N)) * 1 / np.sqrt(R) / fr[:, None], "e5m2")
    return {
        "xt_words": xtp[0],
        "xt_scales": xtp[1],
        "w_words": wp[0],
        "w_scales": wp[1],
        "wb_words": wbp[0],
        "wb_scales": wbp[1],
        "old": (1.0 * n((N, C))).astype(np.float32),
        "offs": striped8(idx),
        "offs2": striped(idx2),
    }


def reference(xt_words, xt_scales, w_words, w_scales, wb_words, wb_scales, old, offs, offs2):
    idx = unstriped8(offs)
    idx2 = unstriped(offs2)
    xtu = unpack_weight(xt_words, xt_scales, "e4m3")
    wu = unpack_weight(w_words, w_scales, "e2m1")
    wbu = unpack_weight(wb_words, wb_scales, "e5m2")
    xtidxg = pick8(xtu, idx, 64)
    a = wu.T @ xtidxg
    hid = a.reshape(R, G, J // G).max(axis=2)
    hidq = mxq(hid, 0, "e5m2")
    p = wbu.T @ hidq
    pp = np.zeros((N, C))
    pp[:, idx2] = p
    y = pp + 0.5 * f64(old)
    return y

@@ -1,0 +1,175 @@
+from contextlib import ExitStack
+
+import concourse.mybir as mybir
+
+K, T, J, R, G, N, C = 1024, 512, 256, 512, 128, 256, 1024
+FLOPS = 2 * K * R * J + 2 * R * N * G
+
+F32 = mybir.dt.float32
+BF16 = mybir.dt.bfloat16
+I32 = mybir.dt.int32
+U32 = mybir.dt.uint32
+U16 = mybir.dt.uint16
+U8 = mybir.dt.uint8
+E4M3X4 = mybir.dt.float8_e4m3fn_x4
+E5M2X4 = mybir.dt.float8_e5m2_x4
+E2M1X4 = mybir.dt.float4_e2m1fn_x4
+ALU = mybir.AluOpType
+COPY = mybir.ActivationFunctionType.Copy
+
+P = 128
+PACK = 4
+PASSES = K // (P * PACK)
+QUADS = 4
+CHUNK = 512
+HALF = J // 2
+
+
+def tile_list_headpicks_pooled_scattered_kernel(
+    tc, xt_words, xt_scales, w_words, w_scales, wb_words, wb_scales, old, offs, offs2, out
+):
+    nc = tc.nc
+    with ExitStack() as ctx:
+        lists = ctx.enter_context(tc.tile_pool(name="lists", bufs=1))
+        keep = ctx.enter_context(tc.tile_pool(name="keep", bufs=1))
+        psum = ctx.enter_context(tc.psum_pool(name="psum", bufs=1))
+
+        picks = lists.tile([P, J // 16], U16, name="picks")
+        places = lists.tile([P, G // 16], U16, name="places")
+
+        x_scale_rows = keep.tile([P, T], U8, name="x_scale_rows", align_bytes=64)
+        w_scale_rows = keep.tile([P, R], U8, name="w_scale_rows", align_bytes=64)
+        rider = [R, P]
+        staged = [keep.tile([P, HALF + rider[h]], U8, name="staged%d" % h, align_bytes=64) for h in range(2)]
+        planes = [keep.tile([P, PASSES, HALF + rider[h]], U8, name="planes%d" % h, align_bytes=64) for h in range(2)]
+        nc.sync.dma_start(picks[:], offs)
+        nc.sync.dma_start(places[:], offs2)
+        for rows, source in ((x_scale_rows, xt_scales), (w_scale_rows, w_scales)):
+            nc.vector.memset(rows[:].bitcast(I32), 0)
+            nc.scalar.dma_start(
+                out=rows[0:P:4, :].bitcast(I32), in_=source.rearrange("z q c -> q z c").bitcast(I32)
+            )
+        nc.scalar.dma_start(
+            out=staged[1][0:P:4, HALF:].bitcast(I32),
+            in_=wb_scales[0].rearrange("q (i n) -> (q i) n", i=N // P).bitcast(I32),
+        )
+        for h in range(2):
+            nc.vector.memset(planes[h][:].rearrange("p z c -> p (z c)").bitcast(I32), 0)
+
+        x_table = [
+            keep.tile([P, T], I32, name="x_table%d" % z, tag="slot_b%d" % z, align_bytes=64) for z in range(PASSES)
+        ]
+        w_raw = keep.tile([P, PASSES, 2 * R], U8, name="w_raw", align_bytes=64)
+        nc.sync.dma_start(out=x_table[0][:], in_=xt_words[0].rearrange("p c r -> p (c r)").bitcast(I32))
+        nc.sync.dma_start(out=w_raw[:].bitcast(I32), in_=w_words.rearrange("z p c -> p z c").bitcast(I32))
+        nc.sync.dma_start(out=x_table[1][:], in_=xt_words[1].rearrange("p c r -> p (c r)").bitcast(I32))
+
+        pages = []
+        for i in range(N // P):
+            page = keep.tile([P, C], F32, name="page%d" % i)
+            nc.vector.memset(page[:], 0.0)
+            pages.append(page)
+
+        half_picks = [picks[:, HALF // 16 * h : HALF // 16 * (h + 1)] for h in range(2)]
+        for h in range(2):
+            x_scale_picked = keep.tile([P, HALF], U8, name="x_scale_picked%d" % h, tag="slot_c%d" % h, align_bytes=64)
+            nc.vector.tensor_copy(x_scale_picked[:], x_scale_rows[:].indirect(half_picks[h]))
+            if h == 0:
+                nc.vector.tensor_copy(
+                    staged[0][:, HALF:].rearrange("p (t m) -> p t m", t=PACK),
+                    w_scale_rows[:].rearrange("p (m t) -> p t m", t=PACK),
+                )
+            nc.vector.tensor_copy(staged[h][:, 0:HALF].bitcast(I32), x_scale_picked[:].bitcast(I32))
+            for quad in range(QUADS):
+                queue = nc.scalar if quad % 2 == 0 else nc.sync
+                queue.dma_start(
+                    out=planes[h][32 * quad : 32 * quad + 4, :, :].bitcast(I32),
+                    in_=staged[h][32 * quad : 32 * quad + 32 : 4, :].bitcast(I32),
+                )
+
+        x_picked, w_codes = {}, []
+
+        def pick_words(h, z):
+            picked = keep.tile([P, HALF], U32, name="x_picked%d_%d" % (h, z), align_bytes=64)
+            nc.vector.tensor_copy(picked[:], x_table[z][:].bitcast(U32).indirect(half_picks[h]))
+            x_picked[h, z] = picked
+
+        for z in range(PASSES):
+            pick_words(0, z)
+            codes = keep.tile([P, 2 * R], U8, name="w_codes%d" % z, align_bytes=64)
+            nc.vector.tensor_copy(
+                codes[:].bitcast(U16).rearrange("p (t m) -> p t m", t=PACK),
+                w_raw[:, z, :].bitcast(U16).rearrange("p (m t) -> p t m", t=PACK),
+            )
+            w_codes.append(codes)
+        for z in range(PASSES):
+            pick_words(1, z)
+
+        wb_codes = keep.tile([P, N], I32, name="wb_codes", tag="slot_b0", align_bytes=64)
+        nc.sync.dma_start(out=wb_codes[:], in_=wb_words[0].rearrange("p c r -> p (c r)").bitcast(I32))
+        old_rows = keep.tile([P, N // P, C], F32, name="old_rows", tag="slot_c1", align_bytes=64)
+        nc.sync.dma_start(out=old_rows[:], in_=old.rearrange("(i p) c -> p i c", p=P))
+
+        hid = keep.tile([P, G, PACK], BF16, name="hid", align_bytes=64)
+        hid_codes = keep.tile([P, G], U32, name="hid_codes", align_bytes=64)
+        hid_plane = keep.tile([P, G], U8, name="hid_plane", align_bytes=64)
+        for h in range(2):
+            banks = [psum.tile([P, 2, HALF], F32, name="a_bank%d_%d" % (h, b)) for b in range(2)]
+            for z in range(PASSES):
+                for t in range(PACK):
+                    nc.tensor.matmul_mx(
+                        out=banks[t // 2][:, t % 2, :],
+                        lhsT=w_codes[z][:, 2 * P * t : 2 * P * (t + 1)].bitcast(E2M1X4),
+                        lhsT_scale=planes[0][:, z, HALF + P * t : HALF + P * (t + 1)],
+                        rhs=x_picked[h, z][:].bitcast(E4M3X4),
+                        rhs_scale=planes[h][:, z, 0:HALF],
+                        start=(z == 0 and t % 2 == 0),
+                        stop=(z == PASSES - 1 and t % 2 == 1),
+                    )
+            pairs = slice(G // 2 * h, G // 2 * (h + 1))
+            for b in range(2):
+                nc.vector.tensor_reduce(
+                    out=hid[:, pairs, 2 * b : 2 * b + 2],
+                    in_=banks[b][:].rearrange("p t (g e) -> p g t e", e=2),
+                    axis=mybir.AxisListType.X,
+                    op=ALU.max,
+                )
+            nc.vector.quantize_mx(
+                out=hid_codes[:, pairs].bitcast(E5M2X4),
+                scales=hid_plane[:, pairs],
+                in_=hid[:, pairs, :].rearrange("p g t -> p (g t)"),
+            )
+
+        products = []
+        for i in range(N // P):
+            p_bank = psum.tile([P, G], F32, name="p_bank%d" % i)
+            nc.tensor.matmul_mx(
+                out=p_bank[:],
+                lhsT=wb_codes[:, P * i : P * (i + 1)].bitcast(E5M2X4),
+                lhsT_scale=planes[1][:, i, HALF:],
+                rhs=hid_codes[:].bitcast(E5M2X4),
+                rhs_scale=hid_plane[:],
+                start=True,
+                stop=True,
+            )
+            product = keep.tile([P, G], F32, name="product%d" % i)
+            if i == 0:
+                nc.vector.tensor_copy(product[:], p_bank[:])
+            else:
+                nc.scalar.activation(product[:], p_bank[:], COPY)
+            products.append(product)
+        nc.scalar.activation(pages[0][:].indirect(places[:]), products[0][:], COPY)
+        nc.vector.tensor_copy(pages[1][:].indirect(places[:]), products[1][:])
+
+        for i in range(N // P):
+            for c0 in range(0, C, CHUNK):
+                result = keep.tile([P, CHUNK], F32, name="result%d_%d" % (i, c0))
+                nc.vector.scalar_tensor_tensor(
+                    out=result[:],
+                    in0=old_rows[:, i, c0 : c0 + CHUNK],
+                    scalar=0.5,
+                    in1=pages[i][:, c0 : c0 + CHUNK],
+                    op0=ALU.mult,
+                    op1=ALU.add,
+                )
+                nc.sync.dma_start(out=out[P * i : P * (i + 1), c0 : c0 + CHUNK], in_=result[:])

@@ -37,57 +37,46 @@ def tile_list_headpicks_pooled_scattered_kernel(
         picks = lists.tile([P, J // 16], U16, name="picks")
         places = lists.tile([P, G // 16], U16, name="places")
 
-        x_scale_rows = keep.tile([P, T], U8, name="x_scale_rows", align_bytes=64)
-        w_scale_rows = keep.tile([P, R], U8, name="w_scale_rows", align_bytes=64)
-        rider = [R, P]
-        staged = [keep.tile([P, HALF + rider[h]], U8, name="staged%d" % h, align_bytes=64) for h in range(2)]
-        planes = [keep.tile([P, PASSES, HALF + rider[h]], U8, name="planes%d" % h, align_bytes=64) for h in range(2)]
+        x_scale_rows = keep.tile([P, T], U8, name="x_scale_rows", tag="slot_a", align_bytes=64)
+        w_scale_rows = keep.tile([P, PASSES, R], U8, name="w_scale_rows", tag="slot_d", align_bytes=64)
+        x_plane = keep.tile([P, PASSES, J], U8, name="x_plane", align_bytes=64)
         nc.sync.dma_start(picks[:], offs)
         nc.sync.dma_start(places[:], offs2)
-        for rows, source in ((x_scale_rows, xt_scales), (w_scale_rows, w_scales)):
-            nc.vector.memset(rows[:].bitcast(I32), 0)
-            nc.scalar.dma_start(
-                out=rows[0:P:4, :].bitcast(I32), in_=source.rearrange("z q c -> q z c").bitcast(I32)
-            )
-        nc.scalar.dma_start(
-            out=staged[1][0:P:4, HALF:].bitcast(I32),
-            in_=wb_scales[0].rearrange("q (i n) -> (q i) n", i=N // P).bitcast(I32),
+        nc.vector.memset(x_scale_rows[:].bitcast(I32), 0)
+        nc.sync.dma_start(
+            out=x_scale_rows[0:P:4, :].bitcast(I32),
+            in_=xt_scales.rearrange("z q c -> q z c").bitcast(I32),
         )
-        for h in range(2):
-            nc.vector.memset(planes[h][:].rearrange("p z c -> p (z c)").bitcast(I32), 0)
+        nc.vector.memset(w_scale_rows[:].rearrange("p z r -> p (z r)").bitcast(I32), 0)
+        for quad in range(QUADS):
+            nc.scalar.dma_start(
+                out=w_scale_rows[32 * quad : 32 * quad + 4, :, :].bitcast(I32),
+                in_=w_scales[:, 4 * quad : 4 * quad + 4, :].rearrange("z q c -> q z c").bitcast(I32),
+            )
+        nc.vector.memset(x_plane[:].rearrange("p z j -> p (z j)").bitcast(I32), 0)
 
         x_table = [
             keep.tile([P, T], I32, name="x_table%d" % z, tag="slot_b%d" % z, align_bytes=64) for z in range(PASSES)
         ]
-        w_raw = keep.tile([P, PASSES, 2 * R], U8, name="w_raw", align_bytes=64)
+        w_raw = keep.tile([P, PASSES, 2 * R], U8, name="w_raw", tag="slot_c", align_bytes=64)
         nc.sync.dma_start(out=x_table[0][:], in_=xt_words[0].rearrange("p c r -> p (c r)").bitcast(I32))
         nc.sync.dma_start(out=w_raw[:].bitcast(I32), in_=w_words.rearrange("z p c -> p z c").bitcast(I32))
         nc.sync.dma_start(out=x_table[1][:], in_=xt_words[1].rearrange("p c r -> p (c r)").bitcast(I32))
 
-        pages = []
-        for i in range(N // P):
-            page = keep.tile([P, C], F32, name="page%d" % i)
-            nc.vector.memset(page[:], 0.0)
-            pages.append(page)
+        pages = [keep.tile([P, C], F32, name="page0")]
+        nc.vector.memset(pages[0][:], 0.0)
+
+        x_scale_picked = keep.tile([P, J], U8, name="x_scale_picked", align_bytes=64)
+        nc.vector.tensor_copy(x_scale_picked[:], x_scale_rows[:].indirect(picks[:]))
+        for quad in range(QUADS):
+            queue = nc.scalar if quad % 2 == 0 else nc.sync
+            queue.dma_start(
+                out=x_plane[32 * quad : 32 * quad + 4, :, :].bitcast(I32),
+                in_=x_scale_picked[32 * quad : 32 * quad + 32 : 4, :].bitcast(I32),
+            )
 
         half_picks = [picks[:, HALF // 16 * h : HALF // 16 * (h + 1)] for h in range(2)]
-        for h in range(2):
-            x_scale_picked = keep.tile([P, HALF], U8, name="x_scale_picked%d" % h, tag="slot_c%d" % h, align_bytes=64)
-            nc.vector.tensor_copy(x_scale_picked[:], x_scale_rows[:].indirect(half_picks[h]))
-            if h == 0:
-                nc.vector.tensor_copy(
-                    staged[0][:, HALF:].rearrange("p (t m) -> p t m", t=PACK),
-                    w_scale_rows[:].rearrange("p (m t) -> p t m", t=PACK),
-                )
-            nc.vector.tensor_copy(staged[h][:, 0:HALF].bitcast(I32), x_scale_picked[:].bitcast(I32))
-            for quad in range(QUADS):
-                queue = nc.scalar if quad % 2 == 0 else nc.sync
-                queue.dma_start(
-                    out=planes[h][32 * quad : 32 * quad + 4, :, :].bitcast(I32),
-                    in_=staged[h][32 * quad : 32 * quad + 32 : 4, :].bitcast(I32),
-                )
-
-        x_picked, w_codes = {}, []
+        x_picked, w_codes, w_planes = {}, [], []
 
         def pick_words(h, z):
             picked = keep.tile([P, HALF], U32, name="x_picked%d_%d" % (h, z), align_bytes=64)
@@ -102,13 +91,30 @@ def tile_list_headpicks_pooled_scattered_kernel(
                 w_raw[:, z, :].bitcast(U16).rearrange("p (m t) -> p t m", t=PACK),
             )
             w_codes.append(codes)
+            plane = keep.tile([P, R], U8, name="w_plane%d" % z, align_bytes=64)
+            nc.vector.tensor_copy(
+                plane[:].rearrange("p (t m) -> p t m", t=PACK),
+                w_scale_rows[:, z, :].rearrange("p (m t) -> p t m", t=PACK),
+            )
+            w_planes.append(plane)
         for z in range(PASSES):
             pick_words(1, z)
 
-        wb_codes = keep.tile([P, N], I32, name="wb_codes", tag="slot_b0", align_bytes=64)
+        wb_plane = keep.tile([P, N], U8, name="wb_plane", tag="slot_a", align_bytes=64)
+        nc.vector.memset(wb_plane[:].bitcast(I32), 0)
+        for quad in range(QUADS):
+            queue = nc.scalar if quad % 2 == 0 else nc.sync
+            queue.dma_start(
+                out=wb_plane[32 * quad : 32 * quad + 4, :].bitcast(I32),
+                in_=wb_scales[0, 4 * quad : 4 * quad + 4, :].bitcast(I32),
+            )
+        wb_codes = keep.tile([P, N], I32, name="wb_codes", tag="slot_d", align_bytes=64)
         nc.sync.dma_start(out=wb_codes[:], in_=wb_words[0].rearrange("p c r -> p (c r)").bitcast(I32))
-        old_rows = keep.tile([P, N // P, C], F32, name="old_rows", tag="slot_c1", align_bytes=64)
+        old_rows = keep.tile([P, N // P, C], F32, name="old_rows", tag="slot_c", align_bytes=64)
         nc.sync.dma_start(out=old_rows[:], in_=old.rearrange("(i p) c -> p i c", p=P))
+
+        pages.append(keep.tile([P, C], F32, name="page1", tag="slot_b1", align_bytes=64))
+        nc.gpsimd.memset(pages[1][:], 0.0)
 
         hid = keep.tile([P, G, PACK], BF16, name="hid", align_bytes=64)
         hid_codes = keep.tile([P, G], U32, name="hid_codes", align_bytes=64)
@@ -120,9 +126,9 @@ def tile_list_headpicks_pooled_scattered_kernel(
                     nc.tensor.matmul_mx(
                         out=banks[t // 2][:, t % 2, :],
                         lhsT=w_codes[z][:, 2 * P * t : 2 * P * (t + 1)].bitcast(E2M1X4),
-                        lhsT_scale=planes[0][:, z, HALF + P * t : HALF + P * (t + 1)],
+                        lhsT_scale=w_planes[z][:, P * t : P * (t + 1)],
                         rhs=x_picked[h, z][:].bitcast(E4M3X4),
-                        rhs_scale=planes[h][:, z, 0:HALF],
+                        rhs_scale=x_plane[:, z, HALF * h : HALF * (h + 1)],
                         start=(z == 0 and t % 2 == 0),
                         stop=(z == PASSES - 1 and t % 2 == 1),
                     )
@@ -146,7 +152,7 @@ def tile_list_headpicks_pooled_scattered_kernel(
             nc.tensor.matmul_mx(
                 out=p_bank[:],
                 lhsT=wb_codes[:, P * i : P * (i + 1)].bitcast(E5M2X4),
-                lhsT_scale=planes[1][:, i, HALF:],
+                lhsT_scale=wb_plane[:, P * i : P * (i + 1)],
                 rhs=hid_codes[:].bitcast(E5M2X4),
                 rhs_scale=hid_plane[:],
                 start=True,

from contextlib import ExitStack

import concourse.mybir as mybir

K, T, J, R, G, N, C = 1024, 512, 256, 512, 128, 256, 1024
FLOPS = 2 * K * R * J + 2 * R * N * G

F32 = mybir.dt.float32
BF16 = mybir.dt.bfloat16
I32 = mybir.dt.int32
U32 = mybir.dt.uint32
U16 = mybir.dt.uint16
U8 = mybir.dt.uint8
E4M3X4 = mybir.dt.float8_e4m3fn_x4
E5M2X4 = mybir.dt.float8_e5m2_x4
E2M1X4 = mybir.dt.float4_e2m1fn_x4
ALU = mybir.AluOpType
COPY = mybir.ActivationFunctionType.Copy

P = 128
PACK = 4
PASSES = K // (P * PACK)
QUADS = 4
CHUNK = 512
HALF = J // 2


def tile_list_headpicks_pooled_scattered_kernel(
    tc, xt_words, xt_scales, w_words, w_scales, wb_words, wb_scales, old, offs, offs2, out
):
    nc = tc.nc
    with ExitStack() as ctx:
        lists = ctx.enter_context(tc.tile_pool(name="lists", bufs=1))
        keep = ctx.enter_context(tc.tile_pool(name="keep", bufs=1))
        psum = ctx.enter_context(tc.psum_pool(name="psum", bufs=1))

        picks = lists.tile([P, J // 16], U16, name="picks")
        places = lists.tile([P, G // 16], U16, name="places")

        x_scale_rows = keep.tile([P, T], U8, name="x_scale_rows", tag="slot_a", align_bytes=64)
        w_scale_rows = keep.tile([P, PASSES, R], U8, name="w_scale_rows", tag="slot_d", align_bytes=64)
        x_plane = keep.tile([P, PASSES, J], U8, name="x_plane", align_bytes=64)
        nc.sync.dma_start(picks[:], offs)
        nc.sync.dma_start(places[:], offs2)
        nc.vector.memset(x_scale_rows[:].bitcast(I32), 0)
        nc.sync.dma_start(
            out=x_scale_rows[0:P:4, :].bitcast(I32),
            in_=xt_scales.rearrange("z q c -> q z c").bitcast(I32),
        )
        nc.vector.memset(w_scale_rows[:].rearrange("p z r -> p (z r)").bitcast(I32), 0)
        for quad in range(QUADS):
            nc.scalar.dma_start(
                out=w_scale_rows[32 * quad : 32 * quad + 4, :, :].bitcast(I32),
                in_=w_scales[:, 4 * quad : 4 * quad + 4, :].rearrange("z q c -> q z c").bitcast(I32),
            )
        nc.vector.memset(x_plane[:].rearrange("p z j -> p (z j)").bitcast(I32), 0)

        x_table = [
            keep.tile([P, T], I32, name="x_table%d" % z, tag="slot_b%d" % z, align_bytes=64) for z in range(PASSES)
        ]
        w_raw = keep.tile([P, PASSES, 2 * R], U8, name="w_raw", tag="slot_c", align_bytes=64)
        nc.sync.dma_start(out=x_table[0][:], in_=xt_words[0].rearrange("p c r -> p (c r)").bitcast(I32))
        nc.sync.dma_start(out=w_raw[:].bitcast(I32), in_=w_words.rearrange("z p c -> p z c").bitcast(I32))
        nc.sync.dma_start(out=x_table[1][:], in_=xt_words[1].rearrange("p c r -> p (c r)").bitcast(I32))

        pages = [keep.tile([P, C], F32, name="page0")]
        nc.vector.memset(pages[0][:], 0.0)

        x_scale_picked = keep.tile([P, J], U8, name="x_scale_picked", align_bytes=64)
        nc.vector.tensor_copy(x_scale_picked[:], x_scale_rows[:].indirect(picks[:]))
        for quad in range(QUADS):
            queue = nc.scalar if quad % 2 == 0 else nc.sync
            queue.dma_start(
                out=x_plane[32 * quad : 32 * quad + 4, :, :].bitcast(I32),
                in_=x_scale_picked[32 * quad : 32 * quad + 32 : 4, :].bitcast(I32),
            )

        half_picks = [picks[:, HALF // 16 * h : HALF // 16 * (h + 1)] for h in range(2)]
        x_picked, w_codes, w_planes = {}, [], []

        def pick_words(h, z):
            picked = keep.tile([P, HALF], U32, name="x_picked%d_%d" % (h, z), align_bytes=64)
            nc.vector.tensor_copy(picked[:], x_table[z][:].bitcast(U32).indirect(half_picks[h]))
            x_picked[h, z] = picked

        for z in range(PASSES):
            pick_words(0, z)
            codes = keep.tile([P, 2 * R], U8, name="w_codes%d" % z, align_bytes=64)
            nc.vector.tensor_copy(
                codes[:].bitcast(U16).rearrange("p (t m) -> p t m", t=PACK),
                w_raw[:, z, :].bitcast(U16).rearrange("p (m t) -> p t m", t=PACK),
            )
            w_codes.append(codes)
            plane = keep.tile([P, R], U8, name="w_plane%d" % z, align_bytes=64)
            nc.vector.tensor_copy(
                plane[:].rearrange("p (t m) -> p t m", t=PACK),
                w_scale_rows[:, z, :].rearrange("p (m t) -> p t m", t=PACK),
            )
            w_planes.append(plane)
        for z in range(PASSES):
            pick_words(1, z)

        wb_plane = keep.tile([P, N], U8, name="wb_plane", tag="slot_a", align_bytes=64)
        nc.vector.memset(wb_plane[:].bitcast(I32), 0)
        for quad in range(QUADS):
            queue = nc.scalar if quad % 2 == 0 else nc.sync
            queue.dma_start(
                out=wb_plane[32 * quad : 32 * quad + 4, :].bitcast(I32),
                in_=wb_scales[0, 4 * quad : 4 * quad + 4, :].bitcast(I32),
            )
        wb_codes = keep.tile([P, N], I32, name="wb_codes", tag="slot_d", align_bytes=64)
        nc.sync.dma_start(out=wb_codes[:], in_=wb_words[0].rearrange("p c r -> p (c r)").bitcast(I32))
        old_rows = keep.tile([P, N // P, C], F32, name="old_rows", tag="slot_c", align_bytes=64)
        nc.sync.dma_start(out=old_rows[:], in_=old.rearrange("(i p) c -> p i c", p=P))

        pages.append(keep.tile([P, C], F32, name="page1", tag="slot_b1", align_bytes=64))
        nc.gpsimd.memset(pages[1][:], 0.0)

        hid = keep.tile([P, G, PACK], BF16, name="hid", align_bytes=64)
        hid_codes = keep.tile([P, G], U32, name="hid_codes", align_bytes=64)
        hid_plane = keep.tile([P, G], U8, name="hid_plane", align_bytes=64)
        for h in range(2):
            banks = [psum.tile([P, 2, HALF], F32, name="a_bank%d_%d" % (h, b)) for b in range(2)]
            for z in range(PASSES):
                for t in range(PACK):
                    nc.tensor.matmul_mx(
                        out=banks[t // 2][:, t % 2, :],
                        lhsT=w_codes[z][:, 2 * P * t : 2 * P * (t + 1)].bitcast(E2M1X4),
                        lhsT_scale=w_planes[z][:, P * t : P * (t + 1)],
                        rhs=x_picked[h, z][:].bitcast(E4M3X4),
                        rhs_scale=x_plane[:, z, HALF * h : HALF * (h + 1)],
                        start=(z == 0 and t % 2 == 0),
                        stop=(z == PASSES - 1 and t % 2 == 1),
                    )
            pairs = slice(G // 2 * h, G // 2 * (h + 1))
            for b in range(2):
                nc.vector.tensor_reduce(
                    out=hid[:, pairs, 2 * b : 2 * b + 2],
                    in_=banks[b][:].rearrange("p t (g e) -> p g t e", e=2),
                    axis=mybir.AxisListType.X,
                    op=ALU.max,
                )
            nc.vector.quantize_mx(
                out=hid_codes[:, pairs].bitcast(E5M2X4),
                scales=hid_plane[:, pairs],
                in_=hid[:, pairs, :].rearrange("p g t -> p (g t)"),
            )

        products = []
        for i in range(N // P):
            p_bank = psum.tile([P, G], F32, name="p_bank%d" % i)
            nc.tensor.matmul_mx(
                out=p_bank[:],
                lhsT=wb_codes[:, P * i : P * (i + 1)].bitcast(E5M2X4),
                lhsT_scale=wb_plane[:, P * i : P * (i + 1)],
                rhs=hid_codes[:].bitcast(E5M2X4),
                rhs_scale=hid_plane[:],
                start=True,
                stop=True,
            )
            product = keep.tile([P, G], F32, name="product%d" % i)
            if i == 0:
                nc.vector.tensor_copy(product[:], p_bank[:])
            else:
                nc.scalar.activation(product[:], p_bank[:], COPY)
            products.append(product)
        nc.scalar.activation(pages[0][:].indirect(places[:]), products[0][:], COPY)
        nc.vector.tensor_copy(pages[1][:].indirect(places[:]), products[1][:])

        for i in range(N // P):
            for c0 in range(0, C, CHUNK):
                result = keep.tile([P, CHUNK], F32, name="result%d_%d" % (i, c0))
                nc.vector.scalar_tensor_tensor(
                    out=result[:],
                    in0=old_rows[:, i, c0 : c0 + CHUNK],
                    scalar=0.5,
                    in1=pages[i][:, c0 : c0 + CHUNK],
                    op0=ALU.mult,
                    op1=ALU.add,
                )
                nc.sync.dma_start(out=out[P * i : P * (i + 1), c0 : c0 + CHUNK], in_=result[:])
